import numpy as np, ml_dtypes
CORES = [2,3,42,43,82,83,122,123]
N = 8
import mx_ref
BF = ml_dtypes.bfloat16
def entries(a):
    return np.ascontiguousarray(a.T).reshape(-1)
def table(e):
    return np.ascontiguousarray(np.reshape(e, (-1, 16)).T).astype(np.int32)
def cols(t, e):
    v = np.concatenate([t.reshape(128, -1, 4), np.zeros((128, 1, 4), BF)], axis=1)
    return np.ascontiguousarray(v[:, e]).reshape(128, -1)
def f(rng, *shape):
    return mx_ref.flush((rng.standard_normal(shape, dtype=np.float32) * np.exp2(rng.integers(-2, 3, shape[:-1] + (1,)))).astype(BF))
def wide(rng, *shape, cols=0):
    v = rng.standard_normal(shape, dtype=np.float32) * np.exp2(rng.integers(-12, 13, shape)).astype(np.float32)
    if cols: v *= np.repeat(np.exp2(rng.integers(-cols, cols + 1, shape[:-2] + (1, shape[-1] // 4))) * (rng.random(shape[:-2] + (1, shape[-1] // 4)) > 0.0625), 4, axis=-1).astype(np.float32)
    return mx_ref.flush(v.astype(BF))
T, KP, TOT, QT = 512, 320, 2048, 8
CAPP, DR, CW = KP // N, T // 16, TOT // N
def counts(rng, lo, hi):
    L, U = [TOT], [TOT]
    for q in range(N)[::-1]:
        L.insert(0, max(q * CW - N * DR, L[0] - hi[q]))
        U.insert(0, min((q - 1) * CW + N * (DR + CAPP + 1), U[0] - lo[q]))
    n, s = [], 0
    for q in range(N):
        n.append(int(rng.integers(max(lo[q], L[q + 1] - s), min(hi[q], U[q + 1] - s) + 1))); s += n[-1]
    return n
def slots(k):
    s, p, g = np.full((N, N, CAPP), -1), np.zeros((N, CW), int), 0
    for q in range(N):
        used = [0] * N
        for c in k[q]:
            r = g % N
            s[q, r, used[r]] = c; p[r, g // N] = q * CAPP + used[r]
            used[r] += 1; g += 1
    return np.stack([table(a) for a in s]), np.stack([table(a) for a in p])
def lists(rng, lo=None, hi=None, front=False):
    n = counts(rng, [3 * T // 8] * N if lo is None else lo, [KP] * N if hi is None else hi)
    k = [np.arange(m) if front else np.sort(rng.choice(T, m, replace=False)) for m in n]
    s, p = slots(k)
    return {"kept": np.stack([table(np.concatenate([a, np.full(KP - len(a), -1)])) for a in k]), "snd": s, "pl": p}
def setup_inputs(rng):
    return {"x": f(rng, N, 128, 4 * T), "qw": f(rng, N, 128, QT * 512), **lists(rng)}
def setup_inputs_few(rng):
    return {**setup_inputs(rng), **lists(rng, [T // 2] * (N - 1) + [1], [KP] * (N - 1) + [N])}
def setup_inputs_front(rng):
    return {**setup_inputs(rng), **lists(rng, front=True)}
def setup_inputs_none(rng):
    return {**setup_inputs(rng), **lists(rng, [0] + [T // 2] * (N - 1), [0] + [KP] * (N - 1))}
def setup_inputs_spread(rng):
    d = setup_inputs(rng); d["x"] = wide(rng, N, 128, 4 * T); return d
def setup_inputs_steep(rng):
    d = {**setup_inputs(rng), **lists(rng, [KP] * 5 + [CW + 1, 1, 1], [KP] * 5 + [CW + N, KP, KP])}
    assert (int((d["kept"][:6] >= 0).sum()) - 1) // N - 5 * (CW // N) == DR + CAPP
    return d
def check_inputs(d):
    b, k = [], []
    for q in range(N):
        e = entries(d["kept"][q]); n = int((e >= 0).sum()); k.append(e[:n])
        if e.min() < -1 or e.max() >= T or (e[:n] < 0).any() or (e[n:] != -1).any() or (np.diff(e[:n]) <= 0).any(): b.append("kept")
    if sum(len(a) for a in k) != TOT: b.append("sum of n_q")
    if b: return b
    g = 0
    for q in range(N):
        a = np.arange(g, g + len(k[q])); g += len(k[q])
        if len(a) == 0: continue
        if np.bincount(a % N).max() > CAPP: b.append("columns of a pair")
        p = a // N - q * TOT // (N * N)
        if p.min() < -DR or p.max() > DR + CAPP: b.append("drift")
    s, p = slots(k)
    if not np.array_equal(s, d["snd"]): b.append("snd")
    if not np.array_equal(p, d["pl"]): b.append("pl")
    return b
def reference(x, qw, kept, snd, pl):
    v = []
    for q in range(N):
        e = entries(kept[q]); v.append(cols(x[q], e[e >= 0]))
    v = np.concatenate(v, axis=1)
    y = np.zeros((N, 128, QT * CW), np.float32)
    for r in range(N):
        C = mx_ref.quantize(cols(v, np.arange(r, TOT, N)))
        for o in range(QT): y[r][:, CW * o:CW * o + CW] = mx_ref.matmul(mx_ref.quantize(qw[r][:, 512 * o:512 * o + 512]), C)
    return {"y": y}

from concourse.bass import DstId, RemoteDMATransfer
from concourse.mybir import dt, AluOpType, ActivationFunctionType

N, TC, KP, CAPP, DR, CW, QT = 8, 512, 320, 40, 32, 256, 8
HALF = N // 2
HS = HALF * CAPP
EARLY = KP - 2 * CAPP
LM = 128

SCRATCH = {
    "xs": ("sbuf", [128, 4 * TC], "bfloat16"),
    "sl": ("sbuf", [128, KP // 16], "int32"),
    "of0": ("sbuf", [128, KP // 16], "uint16"),
    "of1": ("sbuf", [128, KP // 16], "uint16"),
    "of2": ("sbuf", [128, KP // 16], "uint16"),
    "of3": ("sbuf", [128, KP // 16], "uint16"),
    "tf": ("sbuf", [128, 4 * HS], "bfloat16"),
    "tn": ("sbuf", [128, 4 * HS], "bfloat16"),
    "qfc": ("sbuf", [128, HS], "float8_e4m3fn_x4"),
    "qfs": ("sbuf", [128, HS], "uint8"),
    "qnc": ("sbuf", [128, HS], "float8_e4m3fn_x4"),
    "qns": ("sbuf", [128, HS], "uint8"),
    "lc": ("sbuf", [128, KP], "float8_e4m3fn_x4"),
    "ls": ("sbuf", [128, KP], "uint8"),
    "pls": ("sbuf", [128, CW // 16], "int32"),
    "plw": ("sbuf", [128, CW // 16], "int32"),
    "plr": ("sbuf", [128, CW // 16], "int32"),
    "offe": ("sbuf", [128, CW // 16], "uint16"),
    "offl": ("sbuf", [128, CW // 16], "uint16"),
    "qwb": ("sbuf", [128, QT * 512], "bfloat16"),
    "qwc": ("sbuf", [128, QT * 128], "float8_e4m3fn_x4"),
    "qws": ("sbuf", [128, QT * 128], "uint8"),
    "ps": ("psum", [128, 512 * QT], "float32"),
    "rs": ("sbuf", [128, KP * QT], "float32"),
    "ysb": ("sbuf", [128, CW * QT], "float32"),
}
SEMAPHORES = (["xl", "sndl", "pll", "qwa", "qwb_", "own", "early", "late", "sent", "go", "store", "pa", "pb", "pc", "qf", "qn"]
              + ["o%d" % t for t in range(4)] + ["gf%d" % t for t in range(4)] + ["gn%d" % t for t in range(4)]
              + ["%s%d" % (a, o) for a in ("qq", "me", "ce", "ge", "ml", "cl", "gl") for o in range(QT)])

COPY = ActivationFunctionType.Copy


def late_ranks(d, T, topo):
    h = d // HALF * HALF
    return [q for q in range(h, h + HALF) if topo.chip(T.cores[q]) != topo.chip(T.cores[d])]


def first(d, T, topo):
    return (max(late_ranks(d, T, topo)) + 1) % N


def land(d, q, T, topo):
    return CAPP * ((q - first(d, T, topo)) % N)


def rank_program(g, core, T, topo):
    r = T.rank_of(core)
    if r is None:
        return
    S = T.sem
    V, A, P, Y = g.vector, g.scalar, g.tensor, g.sync
    my = r // HALF
    fh = 1 - my
    far = list(range(HALF * fh, HALF * fh + HALF))
    late = late_ranks(r, T, topo)
    mate = [q for q in range(N) if q != r and topo.chip(T.cores[q]) == topo.chip(core)]
    OF = [T.of0, T.of1, T.of2, T.of3]

    p0 = max(0, CW // N * min(late) - DR) // 16 * 16
    p1 = (min(CW, CW // N * max(late) + DR + CAPP + 1) + 15) // 16 * 16
    if p1 <= CW - p0:
        l0, l1, e0, e1 = 0, p1, p1, CW
    else:
        l0, l1, e0, e1 = p0, CW, 0, p0
    le, ll = (e1 - e0) // 16, (l1 - l0) // 16

    for k in range(4):
        Y.dma_start(T.sl[16 * k:16 * k + 16, :], T.snd[:, :]).then_inc(S.sndl, 16)
        A.dma_start(T.sl[16 * k + 64:16 * k + 80, :], T.snd[:, :]).then_inc(S.sndl, 16)
    Y.dma_start(T.xs[:, :], T.x[:, :]).then_inc(S.xl, 16)
    Y.dma_start(T.qwb[:, 0:2048], T.qw[:, 0:2048]).then_inc(S.qwa, 16)
    for k in range(8):
        Y.dma_start(T.pls[16 * k:16 * k + 16, :], T.pl[:, :]).then_inc(S.pll, 16)

    V.wait_ge(S.sndl, 128)
    for t in (2, 0, 3, 1):
        V.tensor_scalar(OF[t][:, :], T.sl[:, :], 4.0, float(t), AluOpType.mult, AluOpType.add).then_inc(S["o%d" % t], 1)

    def gather(tile, h, name, wait):
        c = HS // 16 * h
        for eng, t in ((V, 0), (A, 2), (V, 1), (A, 3)):
            if wait:
                eng.wait_ge(S["o%d" % t], 1)
                if t % 2 == 0:
                    eng.wait_ge(S.xl, 16)
            src = T.xs[:, 0:4 * TC].indirect(OF[t][:, c:c + HS // 16])
            if eng is V:
                V.tensor_copy(tile[:, t:4 * HS:4], src).then_inc(S["%s%d" % (name, t)], 1)
            else:
                A.activation(tile[:, t:4 * HS:4], src, COPY).then_inc(S["%s%d" % (name, t)], 1)

    gather(T.tf, fh, "gf", True)
    for t in range(4):
        V.wait_ge(S["gf%d" % t], 1)
    V.quantize_mx(T.qfc[:, :], T.qfs[:, :], T.tf[:, :]).then_inc(S.qf, 1)
    gather(T.tn, my, "gn", False)
    for t in range(4):
        V.wait_ge(S["gn%d" % t], 1)
    V.quantize_mx(T.qnc[:, :], T.qns[:, :], T.tn[:, :]).then_inc(S.qn, 1)

    def transfer(dst, engs, sem, codes, planes, scale):
        rid, pid = topo.addr(T.cores[dst])[:2]
        a, b = CAPP * (dst % HALF), land(dst, r, T, topo)
        if scale:
            s, d = planes[:, a:a + CAPP], T.ls[:, b:b + CAPP]
        else:
            s, d = codes[:, a:a + CAPP].bitcast(dt.uint8), T.lc[:, b:b + CAPP].bitcast(dt.uint8)
        m = 0
        for e in engs:
            m |= 1 << e
        return RemoteDMATransfer(dst_ids=[DstId(rid=rid, pnc=pid)], dma_engine_mask=m, remote_sem=sem, src=s, dst=d)

    g.wait_ge(S.qf, 1)
    sent = 0
    for scale in (False, True):
        tr = []
        for i, d in enumerate(far):
            e = topo.engines(core, T.cores[d])
            w = len(e) // len(far)
            tr.append(transfer(d, e[w * i:w * i + w], S.early, T.qfc, T.qfs, scale))
            sent += w
        g.remote_dma_fused(tr, local_sem=S.sent)
    g.wait_ge(S.qn, 1)
    for scale in (False, True):
        tr, used = [], []
        for i, d in enumerate(late):
            e = topo.engines(core, T.cores[d])
            w = len(e) // len(late)
            tr.append(transfer(d, e[w * i:w * i + w], S.late, T.qnc, T.qns, scale))
            used += e[w * i:w * i + w]
        for d in mate:
            e = [k for k in topo.engines(core, T.cores[d]) if k not in used]
            tr.append(transfer(d, e, S.early, T.qnc, T.qns, scale))
            used += e
        sent += len(used)
        g.remote_dma_fused(tr, local_sem=S.sent)
    g.sem_inc(S.go, 1)
    n_early = 2 * (8 + 8)
    n_late = 2 * 8

    a, b = CAPP * (r % HALF), land(r, r, T, topo)
    Y.wait_ge(S.qn, 1)
    Y.dma_start(T.lc[:, b:b + CAPP].bitcast(dt.uint8), T.qnc[:, a:a + CAPP].bitcast(dt.uint8)).then_inc(S.own, 16)
    Y.dma_start(T.ls[:, b:b + CAPP], T.qns[:, a:a + CAPP]).then_inc(S.own, 16)
    Y.wait_ge(S.go, 1)
    Y.dma_start(T.qwb[:, 2048:4096], T.qw[:, 2048:4096]).then_inc(S.qwb_, 16)

    def quant_w(o):
        V.quantize_mx(T.qwc[:, 128 * o:128 * o + 128], T.qws[:, 128 * o:128 * o + 128],
                      T.qwb[:, 512 * o:512 * o + 512]).then_inc(S["qq%d" % o], 1)

    V.wait_ge(S.qwa, 16)
    V.wait_ge(S.pll, 128)
    rot = float(CAPP * first(r, T, topo))
    V.tensor_scalar(T.plw[:, :], T.pls[:, :], rot, float(KP), AluOpType.is_lt, AluOpType.mult).then_inc(S.pa, 1)
    quant_w(0)
    quant_w(1)
    V.wait_ge(S.pa, 1)
    V.tensor_tensor(T.plr[:, :], T.pls[:, :], T.plw[:, :], AluOpType.add).then_inc(S.pb, 1)
    quant_w(2)
    quant_w(3)
    V.wait_ge(S.pb, 1)
    V.tensor_scalar(T.offe[:, 0:le], T.plr[:, e0 // 16:e1 // 16], rot, None, AluOpType.subtract).then_inc(S.pc, 1)
    V.tensor_scalar(T.offl[:, 0:ll], T.plr[:, l0 // 16:l1 // 16], rot, None, AluOpType.subtract).then_inc(S.pc, 1)
    V.wait_ge(S.qwb_, 16)
    for o in range(4, QT):
        quant_w(o)

    P.wait_ge(S.own, 32)
    P.wait_ge(S.early, n_early)
    for o in range(QT):
        P.wait_ge(S["qq%d" % o], 1)
        P.matmul_mx(T.ps[:, 512 * o:512 * o + EARLY], T.qwc[:, 128 * o:128 * o + 128], T.qws[:, 128 * o:128 * o + 128],
                    T.lc[:, 0:EARLY], T.ls[:, 0:EARLY], True, True).then_inc(S["me%d" % o], 1)
    P.wait_ge(S.late, n_late)
    for o in range(QT):
        P.wait_ge(S["ce%d" % o], 1)
        P.matmul_mx(T.ps[:, 512 * o:512 * o + LM], T.qwc[:, 128 * o:128 * o + 128], T.qws[:, 128 * o:128 * o + 128],
                    T.lc[:, KP - LM:KP], T.ls[:, KP - LM:KP], True, True).then_inc(S["ml%d" % o], 1)

    def move(eng, out, src, sem):
        if eng is V:
            V.tensor_copy(out, src).then_inc(sem, 1)
        else:
            A.activation(out, src, COPY).then_inc(sem, 1)

    def copy_early(eng, o):
        eng.wait_ge(S["me%d" % o], 1)
        move(eng, T.rs[:, KP * o:KP * o + EARLY], T.ps[:, 512 * o:512 * o + EARLY], S["ce%d" % o])

    def gather_early(eng, o):
        eng.wait_ge(S["ce%d" % o], 1)
        move(eng, T.ysb[:, CW * o + e0:CW * o + e1], T.rs[:, KP * o:KP * o + EARLY].indirect(T.offe[:, 0:le]), S["ge%d" % o])

    def copy_late(eng, o):
        eng.wait_ge(S["ml%d" % o], 1)
        move(eng, T.rs[:, KP * o + EARLY:KP * o + KP], T.ps[:, 512 * o + LM - 2 * CAPP:512 * o + LM], S["cl%d" % o])

    def gather_late(eng, o):
        eng.wait_ge(S["cl%d" % o], 1)
        move(eng, T.ysb[:, CW * o + l0:CW * o + l1], T.rs[:, KP * o:KP * o + KP].indirect(T.offl[:, 0:ll]), S["gl%d" % o])

    for eng, k in ((V, 0), (A, 1)):
        eng.wait_ge(S.pc, 2)
        for cp, ga in ((copy_early, gather_early), (copy_late, gather_late)):
            cp(eng, k)
            for o in range(k, QT - 2, 2):
                cp(eng, o + 2)
                ga(eng, o)
            ga(eng, QT - 2 + k)

    for name, a, b in (("ge", e0, e1), ("gl", l0, l1)):
        for o in range(QT):
            Y.wait_ge(S["%s%d" % (name, o)], 1)
            Y.dma_start(T.y[:, CW * o + a:CW * o + b], T.ysb[:, CW * o + a:CW * o + b]).then_inc(S.store, 16)
    Y.wait_ge(S.store, 16 * 2 * QT)
    g.wait_ge(S.sent, sent)
